import numpy as np, ml_dtypes
CORES = [33,34,161,162,289,290,417,418]
N = 8
DEG, TK, TIMES = 3, 256, 2
MASK = [[0,1,6],[0,1,2],[2,5,6],[1,3,4],[2,4,5],[2,5,6],[0,2,6],[1,5,7]]
def setup_inputs(rng):
    return {"x": rng.standard_normal((N, 128, TK), dtype=np.float32).astype(ml_dtypes.bfloat16), "w": (rng.standard_normal((N, 128, DEG * 128), dtype=np.float32) / np.float32(np.sqrt(128 * DEG / 2))).astype(ml_dtypes.bfloat16)}
def setup_inputs_big(rng):
    d = setup_inputs(rng)
    for k in ("x",): d[k] = (d[k].astype(np.float32) * 1048576.0).astype(d[k].dtype)
    return d
def setup_inputs_small(rng):
    d = setup_inputs(rng)
    for k in ("x",): d[k] = (d[k].astype(np.float32) * (1 / 1048576.0)).astype(d[k].dtype)
    return d
def setup_inputs_apart(rng):
    d = setup_inputs(rng)
    f = (10.0 ** rng.permutation(np.linspace(-1.5, 1.5, N))).astype(np.float32).reshape(N, 1, 1)
    for k in ("x",): d[k] = (d[k].astype(np.float32) * f).astype(d[k].dtype)
    return d
def reference(x, w):
    X, W = x.astype(np.float64), w.astype(np.float64)
    h = list(X)
    for _ in range(TIMES):
        h = [np.maximum(sum(W[r][:, 128 * i:128 * i + 128].T @ h[j] for i, j in enumerate(MASK[r])), 0.0) for r in range(N)]
    return {"y": np.stack(h).astype(ml_dtypes.bfloat16)}

@@ -1,0 +1,272 @@
+from concourse.bass import DstId, RemoteDMATransfer
+from concourse.mybir import AluOpType
+
+N, DEG, TK, M = 8, 3, 256, 128
+WW = DEG * M
+NW = 3
+NB = 4
+
+PROXY = True
+HOME_LATE = True
+NEAR_FWD = True
+ON_SHARE = False
+
+SCRATCH = {
+    "xs": ("sbuf", [128, N * TK], "bfloat16"),
+    "hs": ("sbuf", [128, N * TK], "bfloat16"),
+    "ws": ("sbuf", [128, NW * WW], "bfloat16"),
+    "zero": ("sbuf", [128, TK], "float32"),
+    "yo": ("sbuf", [128, TK], "bfloat16"),
+}
+for _b in range(NB):
+    SCRATCH["ps%d" % _b] = ("psum", [128, 512], "float32")
+SEMAPHORES = ["lx", "lw", "z", "snt", "st", "mf", "rf"]
+for _k in range(N):
+    SEMAPHORES += ["ax%d" % _k, "aw%d" % _k, "ah%d" % _k, "mm%d" % _k, "rl%d" % _k]
+
+
+def _bits(m):
+    return [e for e in range(m.bit_length()) if (m >> e) & 1]
+
+
+def _split(nw, ne):
+    share = 1
+    while share * 2 * nw <= ne:
+        share *= 2
+    out = [share] * nw
+    left = ne - share * nw
+    for i in range(nw):
+        if left >= out[i]:
+            left -= out[i]
+            out[i] *= 2
+    return out
+
+
+def _plan(MASK, cores, topo):
+    R = range(len(cores))
+    size = {"x": 2, "h": 2, "w": 3}
+
+    def ok(a, b):
+        return a == b or topo.may_write(cores[a], cores[b])
+
+    def near(a, b):
+        return a != b and topo.host(cores[a]) == topo.host(cores[b]) and topo.chip(cores[a]) == topo.chip(cores[b])
+
+    cand = {}
+    for j in R:
+        if not PROXY or all(ok(k, j) for k in MASK[j]):
+            cand[j] = [j]
+        else:
+            cand[j] = [p for p in R if ok(j, p) and all(ok(k, p) for k in MASK[j])]
+    late = {p: [j for j in MASK[p] if PROXY and p not in cand[j] and not any(ok(q, p) for q in cand[j])] for p in R}
+    base = {p: set(k for j in late[p] + ([p] if cand[p] == [p] else []) for k in MASK[j]) | {p} for p in R}
+    maker = {j: min(cand[j], key=lambda p: (sum(k not in base[p] for k in MASK[j]), p)) for j in R}
+    sites = {r: [] for r in R}
+    for j in R:
+        sites[maker[j]].append(j)
+    for r in R:
+        sites[r] += late[r]
+        if HOME_LATE and r not in sites[r] and r in MASK[r]:
+            sites[r].append(r)
+    need = {}
+    for r in R:
+        for j in sites[r]:
+            lvl = 2
+            if maker[j] == r and any(j not in sites[u] for u in R if j in MASK[u]):
+                lvl = 0 if j != r else 1
+            for it in [("x", k) for k in MASK[j]] + [("w", j)]:
+                if it[1] != r:
+                    need[it + (r,)] = min(need.get(it + (r,), 2), lvl)
+    hneed = [("h", j, r) for r in R for j in MASK[r] if j not in sites[r]]
+    out = {r: 0 for r in R}
+    for (kind, idx, dst) in need:
+        if ok(idx, dst):
+            out[idx] += size[kind]
+
+    def relay(kind, src, dst, has):
+        c = [m for m in R if m not in (src, dst) and ok(src, m) and ok(m, dst)]
+        m = min(c, key=lambda m: (out[m] == 0, not has(m), out[m], m))
+        out[m] += size[kind]
+        return m
+
+    first, fwd = {r: [] for r in R}, {r: [] for r in R}
+    direct = dict((k, u) for k, u in need.items() if ok(k[1], k[2]))
+    for (kind, idx, dst) in sorted(need):
+        if not ok(idx, dst):
+            m = relay(kind, idx, dst, lambda m: (kind, idx, m) in direct)
+            direct[(kind, idx, m)] = 0
+            fwd[m].append((kind, idx, dst))
+    for (kind, idx, dst), lvl in sorted(direct.items()):
+        via = [m for m in R if near(m, dst) and m != idx and not near(m, idx) and direct.get((kind, idx, m), 2) < 2]
+        if NEAR_FWD and lvl == 2 and via:
+            fwd[via[0]].append((kind, idx, dst))
+        else:
+            first[idx].append((kind, idx, dst, lvl))
+    hs, hfwd = {r: [] for r in R}, {r: [] for r in R}
+    hdirect = set(k for k in hneed if ok(maker[k[1]], k[2]))
+    for (kind, j, dst) in hneed:
+        if (kind, j, dst) not in hdirect:
+            m = relay(kind, maker[j], dst, lambda m: (kind, j, m) in hdirect)
+            hdirect.add((kind, j, m))
+            hfwd[m].append((kind, j, dst))
+    for (kind, j, dst) in sorted(hdirect):
+        hs[maker[j]].append((kind, j, dst))
+    relayed = set((k, i, m) for m in R for (k, i, d) in hfwd[m])
+    later = {r: len([w for w in hs[r] + fwd[r] if not near(r, w[2])]) for r in R}
+    calls = {}
+    for r in R:
+        c = []
+        for lvl in (0, 1, 2):
+            for kind in ("x", "w"):
+                c.append(sorted([w[:3] for w in first[r] if w[0] == kind and w[3] == lvl], key=lambda w: (-later[w[2]], w[2])))
+        c += [[w] for w in fwd[r]]
+        for j in sites[r]:
+            c.append(sorted([w for w in hs[r] if w[1] == j], key=lambda w: (w not in relayed, near(r, w[2]), w[2])))
+        c += [[w] for w in hfwd[r]]
+        calls[r] = [x for x in c if x]
+    return sites, calls
+
+
+def _engines(call, r, cores, topo):
+    me = cores[r]
+    far = None
+    for c in cores:
+        if (topo.host(c), topo.chip(c)) != (topo.host(me), topo.chip(me)) and topo.may_write(me, c):
+            far = _bits(topo.mask(me, c))
+    res = [None] * len(call)
+    offs = [i for i, w in enumerate(call) if _bits(topo.mask(me, cores[w[2]])) == far]
+    ons = [i for i in range(len(call)) if i not in offs]
+    if ON_SHARE and offs:
+        offs, ons = offs + ons, []
+    for idxs, pool in ((offs, far), (ons, None)):
+        if not idxs:
+            continue
+        if pool is None:
+            pool = [e for e in _bits(topo.mask(me, cores[call[idxs[0]][2]])) if e not in far]
+        items = []
+        for i in idxs:
+            if call[i][:2] not in items:
+                items.append(call[i][:2])
+        p = 0
+        for it, n in zip(items, _split(len(items), len(pool))):
+            for i in idxs:
+                if call[i][:2] == it:
+                    res[i] = pool[p:p + n]
+            p += n
+    return res
+
+
+def _schedule(MASK, sites, calls, cores, topo):
+    R = range(len(cores))
+    eta, cnt = {}, {}
+    for r in R:
+        eta[(r, "x", r)] = 0.0
+        eta[(r, "w", r)] = 0.3
+    ptr, tq, busy = [0] * len(cores), [0.0] * len(cores), [0.0] * len(cores)
+    go = True
+    while go:
+        go = False
+        for r in R:
+            while ptr[r] < len(calls[r]) and all((r, w[0], w[1]) in eta for w in calls[r][ptr[r]]):
+                call = calls[r][ptr[r]]
+                t = max([tq[r]] + [eta[(r, w[0], w[1])] for w in call])
+                tq[r] = t + 0.5
+                engs = _engines(call, r, cores, topo)
+                s = max(t + 2.5, busy[r])
+                fin = {}
+                for w, e in zip(call, engs):
+                    assert (w[2], w[0], w[1]) not in eta, w
+                    fin[e[0]] = fin.get(e[0], s) + (1.5 if w[0] == "w" else 1.0) * 8.0 / len(e)
+                    eta[(w[2], w[0], w[1])] = fin[e[0]]
+                    cnt[(w[2], w[0], w[1])] = len(e)
+                    if e[0] == engs[0][0]:
+                        busy[r] = max(busy[r], fin[e[0]])
+                ptr[r] += 1
+                go = True
+            for j in sites[r]:
+                ins = [(r, "x", k) for k in MASK[j]] + [(r, "w", j)]
+                if (r, "h", j) not in eta and all(i in eta for i in ins):
+                    eta[(r, "h", j)] = max(eta[i] for i in ins) + 1.0
+                    go = True
+    assert all(ptr[r] == len(calls[r]) for r in R)
+    return eta, cnt
+
+
+def rank_program(g, core, T, topo):
+    r = T.rank_of(core)
+    if r is None:
+        return
+    MASK, cores, sem = T.tables["MASK"], T.cores, T.sem
+    sites, calls = _plan(MASK, cores, topo)
+    eta, cnt = _schedule(MASK, sites, calls, cores, topo)
+    for q in calls:
+        calls[q].sort(key=lambda c: max(eta[(q, w[0], w[1])] for w in c))
+    eta, cnt = _schedule(MASK, sites, calls, cores, topo)
+
+    def wslot(q, j):
+        return ([q] + [i for i in sites[q] if i != q]).index(j)
+
+    def buf(q, kind, idx):
+        if kind == "x":
+            return T.xs[:, idx * TK:(idx + 1) * TK]
+        if kind == "h":
+            return T.hs[:, idx * TK:(idx + 1) * TK]
+        return T.ws[:, wslot(q, idx) * WW:(wslot(q, idx) + 1) * WW]
+
+    def have(kind, idx):
+        if kind in ("x", "w") and idx == r:
+            return (sem.lx if kind == "x" else sem.lw), 16
+        if kind == "h" and idx in sites[r]:
+            return sem["rl%d" % idx], 1
+        return sem["a%s%d" % (kind, idx)], cnt[(r, kind, idx)]
+
+    g.sync.dma_start(buf(r, "x", r), T.x[:]).then_inc(sem.lx, 16)
+    g.scalar.dma_start(buf(r, "w", r), T.w[:]).then_inc(sem.lw, 16)
+    g.vector.memset(T.zero[:], 0.0).then_inc(sem.z, 1)
+    g.vector.wait_ge(sem.z, 1)
+
+    total = 0
+    for call in calls[r]:
+        for it in sorted(set((w[0], w[1]) for w in call)):
+            g.wait_ge(*have(*it))
+        trs, engs = [], _engines(call, r, cores, topo)
+        for key in sorted(set((e[0], w[0], w[1]) for w, e in zip(call, engs))):
+            ws = [(w, e) for w, e in zip(call, engs) if (e[0], w[0], w[1]) == key]
+            to = [topo.addr(cores[w[2]], core) for w, e in ws]
+            trs.append(RemoteDMATransfer(dst_ids=[DstId(rid=a, pnc=b) for a, b in to],
+                                         dma_engine_mask=sum(1 << b for b in ws[0][1]),
+                                         remote_sem=sem["a%s%d" % key[1:]], srcs=[buf(r, key[1], key[2])],
+                                         dsts=[buf(w[2], w[0], w[1]) for w, e in ws]))
+            total += len(ws[0][1])
+        g.remote_dma_fused(trs, local_sem=sem.snt)
+    if total:
+        g.wait_ge(sem.snt, total)
+
+    mms = []
+    for b, j in enumerate(sites[r]):
+        for i, k in enumerate(MASK[j]):
+            mms.append((max(eta[(r, "x", k)], eta[(r, "w", j)]), b, j, i, ("x", k), ("w", j)))
+    for i, j in enumerate(MASK[r]):
+        mms.append((eta[(r, "h", j)], len(sites[r]), -1, i, ("h", j), ("w", r)))
+    mms.sort()
+    left, seen, order = {}, set(), []
+    for m in mms:
+        left[m[1]] = left.get(m[1], 0) + 1
+    for (t, b, j, i, rhs, lw) in mms:
+        for it in (lw, rhs):
+            if it not in seen:
+                g.tensor.wait_ge(*have(*it))
+                seen.add(it)
+        s = wslot(r, lw[1]) * WW + i * M
+        left[b] -= 1
+        ins = g.tensor.matmul(T["ps%d" % b][:, 0:TK], T.ws[:, s:s + M], buf(r, *rhs), left[b] == DEG - 1, left[b] == 0)
+        if left[b] == 0:
+            ins.then_inc(sem.mf if j < 0 else sem["mm%d" % j], 1)
+            order.append((b, j))
+    for b, j in order:
+        g.vector.wait_ge(sem.mf if j < 0 else sem["mm%d" % j], 1)
+        g.vector.tensor_tensor(T.yo[:] if j < 0 else buf(r, "h", j), T["ps%d" % b][:, 0:TK], T.zero[:],
+                               AluOpType.max).then_inc(sem.rf if j < 0 else sem["rl%d" % j], 1)
+    g.sync.wait_ge(sem.rf, 1)
+    g.sync.dma_start(T.y[:], T.yo[:]).then_inc(sem.st, 16)
+    g.sync.wait_ge(sem.st, 16)

@@ -3,48 +3,31 @@ from concourse.mybir import AluOpType
 
 N, DEG, TK, M = 8, 3, 256, 128
 WW = DEG * M
-NW = 3
-NB = 4
-
-PROXY = True
-HOME_LATE = True
-NEAR_FWD = True
-ON_SHARE = False
+NB = 3
 
 SCRATCH = {
     "xs": ("sbuf", [128, N * TK], "bfloat16"),
     "hs": ("sbuf", [128, N * TK], "bfloat16"),
-    "ws": ("sbuf", [128, NW * WW], "bfloat16"),
+    "ws": ("sbuf", [128, 2 * WW], "bfloat16"),
+    "po": ("sbuf", [128, TK], "bfloat16"),
+    "pi": ("sbuf", [128, TK], "bfloat16"),
     "zero": ("sbuf", [128, TK], "float32"),
     "yo": ("sbuf", [128, TK], "bfloat16"),
 }
 for _b in range(NB):
     SCRATCH["ps%d" % _b] = ("psum", [128, 512], "float32")
-SEMAPHORES = ["lx", "lw", "z", "snt", "st", "mf", "rf"]
+SEMAPHORES = ["lx", "lw", "z", "snt", "st", "rf", "rp", "ad"] + ["mm%d" % _b for _b in range(NB)]
 for _k in range(N):
-    SEMAPHORES += ["ax%d" % _k, "aw%d" % _k, "ah%d" % _k, "mm%d" % _k, "rl%d" % _k]
+    SEMAPHORES += ["ax%d" % _k, "aw%d" % _k, "at%d" % _k, "ap%d" % _k, "ah%d" % _k, "rl%d" % _k]
+SIZE = {"x": 1.0, "h": 1.0, "p": 1.0, "w": 1.5, "t": 0.5}
 
 
 def _bits(m):
     return [e for e in range(m.bit_length()) if (m >> e) & 1]
 
 
-def _split(nw, ne):
-    share = 1
-    while share * 2 * nw <= ne:
-        share *= 2
-    out = [share] * nw
-    left = ne - share * nw
-    for i in range(nw):
-        if left >= out[i]:
-            left -= out[i]
-            out[i] *= 2
-    return out
-
-
 def _plan(MASK, cores, topo):
     R = range(len(cores))
-    size = {"x": 2, "h": 2, "w": 3}
 
     def ok(a, b):
         return a == b or topo.may_write(cores[a], cores[b])
@@ -52,117 +35,94 @@ def _plan(MASK, cores, topo):
     def near(a, b):
         return a != b and topo.host(cores[a]) == topo.host(cores[b]) and topo.chip(cores[a]) == topo.chip(cores[b])
 
-    cand = {}
-    for j in R:
-        if not PROXY or all(ok(k, j) for k in MASK[j]):
-            cand[j] = [j]
-        else:
-            cand[j] = [p for p in R if ok(j, p) and all(ok(k, p) for k in MASK[j])]
-    late = {p: [j for j in MASK[p] if PROXY and p not in cand[j] and not any(ok(q, p) for q in cand[j])] for p in R}
-    base = {p: set(k for j in late[p] + ([p] if cand[p] == [p] else []) for k in MASK[j]) | {p} for p in R}
-    maker = {j: min(cand[j], key=lambda p: (sum(k not in base[p] for k in MASK[j]), p)) for j in R}
-    sites = {r: [] for r in R}
-    for j in R:
-        sites[maker[j]].append(j)
-    for r in R:
-        sites[r] += late[r]
-        if HOME_LATE and r not in sites[r] and r in MASK[r]:
-            sites[r].append(r)
-    need = {}
-    for r in R:
-        for j in sites[r]:
-            lvl = 2
-            if maker[j] == r and any(j not in sites[u] for u in R if j in MASK[u]):
-                lvl = 0 if j != r else 1
-            for it in [("x", k) for k in MASK[j]] + [("w", j)]:
-                if it[1] != r:
-                    need[it + (r,)] = min(need.get(it + (r,), 2), lvl)
-    hneed = [("h", j, r) for r in R for j in MASK[r] if j not in sites[r]]
-    out = {r: 0 for r in R}
-    for (kind, idx, dst) in need:
-        if ok(idx, dst):
-            out[idx] += size[kind]
+    users = {j: [u for u in R if j in MASK[u]] for j in R}
+    hubs = [j for j in R if not all(ok(k, j) for k in MASK[j])]
+    far_tile = {j: [i for i, k in enumerate(MASK[j]) if not ok(k, j)] for j in hubs}
+    assert all(len(far_tile[j]) == 1 for j in hubs)
+    groups = {r: [] for r in R}
+    first, second, third = {r: [] for r in R}, {r: [] for r in R}, {r: [] for r in R}
+    got = set((k, k) for k in R)
 
-    def relay(kind, src, dst, has):
-        c = [m for m in R if m not in (src, dst) and ok(src, m) and ok(m, dst)]
-        m = min(c, key=lambda m: (out[m] == 0, not has(m), out[m], m))
-        out[m] += size[kind]
-        return m
+    def full(j, r):
+        groups[r].append((("h", j), [(("w", j), i, ("x", k)) for i, k in enumerate(MASK[j])], None))
 
-    first, fwd = {r: [] for r in R}, {r: [] for r in R}
-    direct = dict((k, u) for k, u in need.items() if ok(k[1], k[2]))
-    for (kind, idx, dst) in sorted(need):
-        if not ok(idx, dst):
-            m = relay(kind, idx, dst, lambda m: (kind, idx, m) in direct)
-            direct[(kind, idx, m)] = 0
-            fwd[m].append((kind, idx, dst))
-    for (kind, idx, dst), lvl in sorted(direct.items()):
-        via = [m for m in R if near(m, dst) and m != idx and not near(m, idx) and direct.get((kind, idx, m), 2) < 2]
-        if NEAR_FWD and lvl == 2 and via:
-            fwd[via[0]].append((kind, idx, dst))
-        else:
-            first[idx].append((kind, idx, dst, lvl))
-    hs, hfwd = {r: [] for r in R}, {r: [] for r in R}
-    hdirect = set(k for k in hneed if ok(maker[k[1]], k[2]))
-    for (kind, j, dst) in hneed:
-        if (kind, j, dst) not in hdirect:
-            m = relay(kind, maker[j], dst, lambda m: (kind, j, m) in hdirect)
-            hdirect.add((kind, j, m))
-            hfwd[m].append((kind, j, dst))
-    for (kind, j, dst) in sorted(hdirect):
-        hs[maker[j]].append((kind, j, dst))
-    relayed = set((k, i, m) for m in R for (k, i, d) in hfwd[m])
-    later = {r: len([w for w in hs[r] + fwd[r] if not near(r, w[2])]) for r in R}
-    calls = {}
+    maker, split = {}, {}
+    for j in R:
+        if j not in hubs:
+            maker[j] = j
+            continue
+        c = [p for p in R if ok(j, p) and all(ok(k, p) for k in MASK[j])]
+        maker[j] = min(c, key=lambda p: (len([u for u in users[p] if u != p and not near(p, u)]), p))
+        split[j] = [u for u in users[j] if u != j and not ok(maker[j], u)]
     for r in R:
-        c = []
-        for lvl in (0, 1, 2):
-            for kind in ("x", "w"):
-                c.append(sorted([w[:3] for w in first[r] if w[0] == kind and w[3] == lvl], key=lambda w: (-later[w[2]], w[2])))
-        c += [[w] for w in fwd[r]]
-        for j in sites[r]:
-            c.append(sorted([w for w in hs[r] if w[1] == j], key=lambda w: (w not in relayed, near(r, w[2]), w[2])))
-        c += [[w] for w in hfwd[r]]
-        calls[r] = [x for x in c if x]
-    return sites, calls
+        full(r, r)
+    for j in hubs:
+        full(j, maker[j])
+        i = far_tile[j][0]
+        for u in split[j]:
+            groups[u].append((("h", j), [(("t", j), i, ("x", MASK[j][i]))], ("p", j)))
+        if split[j]:
+            groups[j].insert(0, (("p", j), [(("w", j), a, ("x", k)) for a, k in enumerate(MASK[j]) if a != i], None))
+    want = {k: set() for k in R}
+    for r in R:
+        for (out, terms, add) in groups[r]:
+            for (wk, i, rhs) in terms:
+                if rhs[1] != r:
+                    want[rhs[1]].add(r)
+    for k in R:
+        direct = sorted(u for u in want[k] if ok(k, u))
+        if k in hubs:
+            heads = []
+            for u in direct:
+                mate = [v for v in direct if near(u, v)]
+                if not mate or u == maker[k] or (mate[0] != maker[k] and maker.get(MASK[k][far_tile[k][0]]) != u and
+                                                 (maker.get(MASK[k][far_tile[k][0]]) == mate[0] or u < mate[0])):
+                    heads.append(u)
+            heads.sort(key=lambda u: (u != maker[k], u))
+            first[k].append([("x", k, u) for u in heads])
+            relay_to = [u for u in want[k] if not ok(k, u)]
+            for n, u in enumerate(heads):
+                pas = [("x", k, v) for v in direct if near(u, v) and v not in heads]
+                if n == 0:
+                    assert all(ok(u, v) for v in relay_to)
+                    pas = [("x", k, v) for v in relay_to] + pas
+                if pas:
+                    second[u].append(pas)
+            first[k].append([("w", k, maker[k])])
+            for u in split[k]:
+                first[k].append([("t", k, u)])
+                third[k].append([("p", k, u)])
+        elif direct:
+            assert len(direct) == len(want[k])
+            first[k].append([("x", k, u) for u in sorted(direct, key=lambda u: (u not in hubs, near(k, u), u))])
+    for j in R:
+        to = [u for u in users[j] if u != maker[j] and ("h", j) not in [gr[0] for gr in groups[u]]]
+        if to:
+            assert all(ok(maker[j], u) for u in to)
+            third[maker[j]].append([("h", j, u) for u in sorted(to, key=lambda u: (near(maker[j], u), u))])
+    for r in R:
+        groups[r].append((("y", r), [(("w", r), i, ("h", j)) for i, j in enumerate(MASK[r])], None))
+    calls = {r: first[r] + second[r] + third[r] for r in R}
+    for r in R:
+        for c in calls[r]:
+            assert all(ok(r, w[2]) and w[2] != r for w in c)
+    return calls, groups
 
 
 def _engines(call, r, cores, topo):
     me = cores[r]
-    far = None
-    for c in cores:
-        if (topo.host(c), topo.chip(c)) != (topo.host(me), topo.chip(me)) and topo.may_write(me, c):
-            far = _bits(topo.mask(me, c))
-    res = [None] * len(call)
-    offs = [i for i, w in enumerate(call) if _bits(topo.mask(me, cores[w[2]])) == far]
-    ons = [i for i in range(len(call)) if i not in offs]
-    if ON_SHARE and offs:
-        offs, ons = offs + ons, []
-    for idxs, pool in ((offs, far), (ons, None)):
-        if not idxs:
-            continue
-        if pool is None:
-            pool = [e for e in _bits(topo.mask(me, cores[call[idxs[0]][2]])) if e not in far]
-        items = []
-        for i in idxs:
-            if call[i][:2] not in items:
-                items.append(call[i][:2])
-        p = 0
-        for it, n in zip(items, _split(len(items), len(pool))):
-            for i in idxs:
-                if call[i][:2] == it:
-                    res[i] = pool[p:p + n]
-            p += n
-    return res
+    masks = [_bits(topo.mask(me, cores[w[2]])) for w in call]
+    small = min(masks, key=len)
+    return [m if len(m) == len(small) else [e for e in m if e not in small] for m in masks]
 
 
-def _schedule(MASK, sites, calls, cores, topo):
+def _schedule(calls, groups, cores, topo):
     R = range(len(cores))
     eta, cnt = {}, {}
     for r in R:
         eta[(r, "x", r)] = 0.0
-        eta[(r, "w", r)] = 0.3
-    ptr, tq, busy = [0] * len(cores), [0.0] * len(cores), [0.0] * len(cores)
+        eta[(r, "w", r)] = eta[(r, "t", r)] = 0.3
+    ptr, tq, busy = [0] * len(cores), [0.0] * len(cores), [{} for r in R]
     go = True
     while go:
         go = False
@@ -170,25 +130,23 @@ def _schedule(MASK, sites, calls, cores, topo):
             while ptr[r] < len(calls[r]) and all((r, w[0], w[1]) in eta for w in calls[r][ptr[r]]):
                 call = calls[r][ptr[r]]
                 t = max([tq[r]] + [eta[(r, w[0], w[1])] for w in call])
-                tq[r] = t + 0.5
-                engs = _engines(call, r, cores, topo)
-                s = max(t + 2.5, busy[r])
-                fin = {}
-                for w, e in zip(call, engs):
+                tq[r] = t + 0.3
+                for w, e in zip(call, _engines(call, r, cores, topo)):
                     assert (w[2], w[0], w[1]) not in eta, w
-                    fin[e[0]] = fin.get(e[0], s) + (1.5 if w[0] == "w" else 1.0) * 8.0 / len(e)
-                    eta[(w[2], w[0], w[1])] = fin[e[0]]
+                    s = max([t + 1.0] + [busy[r].get(b, 0.0) for b in e]) + SIZE[w[0]] * 8.0 / len(e)
+                    for b in e:
+                        busy[r][b] = s
+                    eta[(w[2], w[0], w[1])] = s
                     cnt[(w[2], w[0], w[1])] = len(e)
-                    if e[0] == engs[0][0]:
-                        busy[r] = max(busy[r], fin[e[0]])
                 ptr[r] += 1
                 go = True
-            for j in sites[r]:
-                ins = [(r, "x", k) for k in MASK[j]] + [(r, "w", j)]
-                if (r, "h", j) not in eta and all(i in eta for i in ins):
-                    eta[(r, "h", j)] = max(eta[i] for i in ins) + 1.0
+            for (out, terms, add) in groups[r]:
+                ins = [(r,) + t[0] for t in terms] + [(r,) + t[2] for t in terms] + ([(r,) + add] if add else [])
+                if (r,) + out not in eta and all(i in eta for i in ins):
+                    eta[(r,) + out] = max(eta[i] for i in ins) + 0.5
                     go = True
     assert all(ptr[r] == len(calls[r]) for r in R)
+    assert all((r,) + gr[0] in eta for r in R for gr in groups[r])
     return eta, cnt
 
 
@@ -197,27 +155,36 @@ def rank_program(g, core, T, topo):
     if r is None:
         return
     MASK, cores, sem = T.tables["MASK"], T.cores, T.sem
-    sites, calls = _plan(MASK, cores, topo)
-    eta, cnt = _schedule(MASK, sites, calls, cores, topo)
+    calls, groups = _plan(MASK, cores, topo)
+    eta, cnt = _schedule(calls, groups, cores, topo)
     for q in calls:
         calls[q].sort(key=lambda c: max(eta[(q, w[0], w[1])] for w in c))
-    eta, cnt = _schedule(MASK, sites, calls, cores, topo)
-
-    def wslot(q, j):
-        return ([q] + [i for i in sites[q] if i != q]).index(j)
+    eta, cnt = _schedule(calls, groups, cores, topo)
+    tile = {}
+    for q in groups:
+        for (out, terms, add) in groups[q]:
+            for (wk, i, rhs) in terms:
+                if wk[0] == "t":
+                    tile[wk[1]] = i
+    made = [gr[0] for gr in groups[r]]
 
     def buf(q, kind, idx):
         if kind == "x":
             return T.xs[:, idx * TK:(idx + 1) * TK]
         if kind == "h":
             return T.hs[:, idx * TK:(idx + 1) * TK]
-        return T.ws[:, wslot(q, idx) * WW:(wslot(q, idx) + 1) * WW]
+        if kind == "p":
+            return T.po[:] if q == idx else T.pi[:]
+        base = 0 if q == idx else WW
+        if kind == "w":
+            return T.ws[:, base:base + WW]
+        return T.ws[:, base + tile[idx] * M:base + (tile[idx] + 1) * M]
 
     def have(kind, idx):
-        if kind in ("x", "w") and idx == r:
+        if kind in ("x", "w", "t") and idx == r:
             return (sem.lx if kind == "x" else sem.lw), 16
-        if kind == "h" and idx in sites[r]:
-            return sem["rl%d" % idx], 1
+        if (kind, idx) in made:
+            return (sem.rp if kind == "p" else sem["rl%d" % idx]), 1
         return sem["a%s%d" % (kind, idx)], cnt[(r, kind, idx)]
 
     g.sync.dma_start(buf(r, "x", r), T.x[:]).then_inc(sem.lx, 16)
@@ -227,46 +194,52 @@ def rank_program(g, core, T, topo):
 
     total = 0
     for call in calls[r]:
-        for it in sorted(set((w[0], w[1]) for w in call)):
-            g.wait_ge(*have(*it))
+        kind, idx = call[0][0], call[0][1]
+        g.wait_ge(*have(kind, idx))
         trs, engs = [], _engines(call, r, cores, topo)
-        for key in sorted(set((e[0], w[0], w[1]) for w, e in zip(call, engs))):
-            ws = [(w, e) for w, e in zip(call, engs) if (e[0], w[0], w[1]) == key]
+        for e0 in sorted(set(e[0] for e in engs)):
+            ws = [(w, e) for w, e in zip(call, engs) if e[0] == e0]
             to = [topo.addr(cores[w[2]], core) for w, e in ws]
             trs.append(RemoteDMATransfer(dst_ids=[DstId(rid=a, pnc=b) for a, b in to],
                                          dma_engine_mask=sum(1 << b for b in ws[0][1]),
-                                         remote_sem=sem["a%s%d" % key[1:]], srcs=[buf(r, key[1], key[2])],
-                                         dsts=[buf(w[2], w[0], w[1]) for w, e in ws]))
+                                         remote_sem=sem["a%s%d" % (kind, idx)], srcs=[buf(r, kind, idx)],
+                                         dsts=[buf(w[2], kind, idx) for w, e in ws]))
             total += len(ws[0][1])
         g.remote_dma_fused(trs, local_sem=sem.snt)
     if total:
         g.wait_ge(sem.snt, total)
 
     mms = []
-    for b, j in enumerate(sites[r]):
-        for i, k in enumerate(MASK[j]):
-            mms.append((max(eta[(r, "x", k)], eta[(r, "w", j)]), b, j, i, ("x", k), ("w", j)))
-    for i, j in enumerate(MASK[r]):
-        mms.append((eta[(r, "h", j)], len(sites[r]), -1, i, ("h", j), ("w", r)))
+    for b, (out, terms, add) in enumerate(groups[r]):
+        for (wk, i, rhs) in terms:
+            mms.append((max(eta[(r,) + wk], eta[(r,) + rhs]), b, i, wk, rhs))
     mms.sort()
-    left, seen, order = {}, set(), []
-    for m in mms:
-        left[m[1]] = left.get(m[1], 0) + 1
-    for (t, b, j, i, rhs, lw) in mms:
-        for it in (lw, rhs):
+    size = [len(gr[1]) for gr in groups[r]]
+    left, seen = list(size), set()
+    for (t, b, i, wk, rhs) in mms:
+        for it in (wk, rhs):
             if it not in seen:
                 g.tensor.wait_ge(*have(*it))
                 seen.add(it)
-        s = wslot(r, lw[1]) * WW + i * M
+        s = (0 if wk[1] == r else WW) + i * M
         left[b] -= 1
-        ins = g.tensor.matmul(T["ps%d" % b][:, 0:TK], T.ws[:, s:s + M], buf(r, *rhs), left[b] == DEG - 1, left[b] == 0)
+        ins = g.tensor.matmul(T["ps%d" % b][:, 0:TK], T.ws[:, s:s + M], buf(r, *rhs), left[b] == size[b] - 1, left[b] == 0)
         if left[b] == 0:
-            ins.then_inc(sem.mf if j < 0 else sem["mm%d" % j], 1)
-            order.append((b, j))
-    for b, j in order:
-        g.vector.wait_ge(sem.mf if j < 0 else sem["mm%d" % j], 1)
-        g.vector.tensor_tensor(T.yo[:] if j < 0 else buf(r, "h", j), T["ps%d" % b][:, 0:TK], T.zero[:],
-                               AluOpType.max).then_inc(sem.rf if j < 0 else sem["rl%d" % j], 1)
+            ins.then_inc(sem["mm%d" % b], 1)
+    for b in sorted(range(len(groups[r])), key=lambda b: eta[(r,) + groups[r][b][0]]):
+        out, terms, add = groups[r][b]
+        ps = T["ps%d" % b][:, 0:TK]
+        g.vector.wait_ge(sem["mm%d" % b], 1)
+        if add:
+            g.vector.wait_ge(*have(*add))
+            g.vector.tensor_tensor(ps, ps, buf(r, *add), AluOpType.add).then_inc(sem.ad, 1)
+            g.vector.wait_ge(sem.ad, 1)
+        if out[0] == "p":
+            g.vector.tensor_copy(buf(r, *out), ps).then_inc(sem.rp, 1)
+        elif out[0] == "y":
+            g.vector.tensor_tensor(T.yo[:], ps, T.zero[:], AluOpType.max).then_inc(sem.rf, 1)
+        else:
+            g.vector.tensor_tensor(buf(r, *out), ps, T.zero[:], AluOpType.max).then_inc(sem["rl%d" % out[1]], 1)
     g.sync.wait_ge(sem.rf, 1)
     g.sync.dma_start(T.y[:], T.yo[:]).then_inc(sem.st, 16)
     g.sync.wait_ge(sem.st, 16)

@@ -3,7 +3,7 @@ from concourse.mybir import AluOpType
 
 N, DEG, TK, M = 8, 3, 256, 128
 WW = DEG * M
-NB = 3
+NB = 4
 
 SCRATCH = {
     "xs": ("sbuf", [128, N * TK], "bfloat16"),
@@ -18,8 +18,8 @@ for _b in range(NB):
     SCRATCH["ps%d" % _b] = ("psum", [128, 512], "float32")
 SEMAPHORES = ["lx", "lw", "z", "snt", "st", "rf", "rp", "ad"] + ["mm%d" % _b for _b in range(NB)]
 for _k in range(N):
-    SEMAPHORES += ["ax%d" % _k, "aw%d" % _k, "at%d" % _k, "ap%d" % _k, "ah%d" % _k, "rl%d" % _k]
-SIZE = {"x": 1.0, "h": 1.0, "p": 1.0, "w": 1.5, "t": 0.5}
+    SEMAPHORES += ["ax%d" % _k, "aw%d" % _k, "at%d" % _k, "ap%d" % _k, "ah%d" % _k, "rl%d" % _k, "aa%d" % _k, "ab%d" % _k]
+SIZE = {"x": 1.0, "h": 1.0, "p": 1.0, "w": 1.5, "t": 0.5, "a": 1.0, "b": 0.5}
 
 
 def _bits(m):
@@ -41,10 +41,9 @@ def _plan(MASK, cores, topo):
     assert all(len(far_tile[j]) == 1 for j in hubs)
     groups = {r: [] for r in R}
     first, second, third = {r: [] for r in R}, {r: [] for r in R}, {r: [] for r in R}
-    got = set((k, k) for k in R)
 
-    def full(j, r):
-        groups[r].append((("h", j), [(("w", j), i, ("x", k)) for i, k in enumerate(MASK[j])], None))
+    def full(j, r, two=False):
+        groups[r].append((("h", j), [((("a" if i < DEG - 1 else "b") if two else "w", j), i, ("x", k)) for i, k in enumerate(MASK[j])], None))
 
     maker, split = {}, {}
     for j in R:
@@ -56,8 +55,11 @@ def _plan(MASK, cores, topo):
         split[j] = [u for u in users[j] if u != j and not ok(maker[j], u)]
     for r in R:
         full(r, r)
+    again = [(j, k) for k in hubs for j in MASK[k] if j not in hubs and set(MASK[j]) <= set(MASK[k]) and ok(j, k)]
+    for (j, k) in again:
+        full(j, k)
     for j in hubs:
-        full(j, maker[j])
+        full(j, maker[j], True)
         i = far_tile[j][0]
         for u in split[j]:
             groups[u].append((("h", j), [(("t", j), i, ("x", MASK[j][i]))], ("p", j)))
@@ -88,13 +90,19 @@ def _plan(MASK, cores, topo):
                     pas = [("x", k, v) for v in relay_to] + pas
                 if pas:
                     second[u].append(pas)
-            first[k].append([("w", k, maker[k])])
+            nb = [v for v in R if near(k, v) and ok(v, maker[k])][0]
+            first[k].append([("b", k, nb)])
+            second[nb].append([("b", k, maker[k])])
+            first[k].append([("a", k, maker[k])])
             for u in split[k]:
                 first[k].append([("t", k, u)])
                 third[k].append([("p", k, u)])
         elif direct:
             assert len(direct) == len(want[k])
             first[k].append([("x", k, u) for u in sorted(direct, key=lambda u: (u not in hubs, near(k, u), u))])
+            for (j, u) in again:
+                if j == k:
+                    first[k].append([("w", k, u)])
     for j in R:
         to = [u for u in users[j] if u != maker[j] and ("h", j) not in [gr[0] for gr in groups[u]]]
         if to:
@@ -109,19 +117,34 @@ def _plan(MASK, cores, topo):
     return calls, groups
 
 
-def _engines(call, r, cores, topo):
+def _link(a, b, topo):
+    if topo.host(a) == topo.host(b) and topo.chip(a) == topo.chip(b):
+        return 0
+    return 1 if topo.rack(topo.host(a)) != topo.rack(topo.host(b)) else 2
+
+
+def _engines(call, r, cores, topo, wide):
     me = cores[r]
-    masks = [_bits(topo.mask(me, cores[w[2]])) for w in call]
-    small = min(masks, key=len)
-    return [m if len(m) == len(small) else [e for e in m if e not in small] for m in masks]
+    leave = min([_bits(topo.mask(me, c)) for c in cores if c != me and topo.mask(me, c)], key=len)
+    out = []
+    for w in call:
+        k, m = _link(me, cores[w[2]], topo), _bits(topo.mask(me, cores[w[2]]))
+        if k == 0:
+            out.append([e for e in m if e not in leave])
+        elif (r, w[0], w[1]) in wide:
+            out.append(m)
+        else:
+            out.append(m[k % 2::2])
+    return out
 
 
-def _schedule(calls, groups, cores, topo):
+def _schedule(calls, groups, cores, topo, wide):
     R = range(len(cores))
-    eta, cnt = {}, {}
+    eta, cnt, iv = {}, {}, {}
     for r in R:
         eta[(r, "x", r)] = 0.0
-        eta[(r, "w", r)] = eta[(r, "t", r)] = 0.3
+        for kd in "wtab":
+            eta[(r, kd, r)] = 0.3
     ptr, tq, busy = [0] * len(cores), [0.0] * len(cores), [{} for r in R]
     go = True
     while go:
@@ -131,13 +154,16 @@ def _schedule(calls, groups, cores, topo):
                 call = calls[r][ptr[r]]
                 t = max([tq[r]] + [eta[(r, w[0], w[1])] for w in call])
                 tq[r] = t + 0.3
-                for w, e in zip(call, _engines(call, r, cores, topo)):
+                for w, e in zip(call, _engines(call, r, cores, topo, wide)):
                     assert (w[2], w[0], w[1]) not in eta, w
-                    s = max([t + 1.0] + [busy[r].get(b, 0.0) for b in e]) + SIZE[w[0]] * 8.0 / len(e)
+                    k = _link(cores[r], cores[w[2]], topo)
+                    b0 = max([t + 1.0] + [busy[r].get(b, 0.0) for b in e])
+                    s = b0 + SIZE[w[0]] * (0.3, 2.0, 0.5)[k]
                     for b in e:
                         busy[r][b] = s
                     eta[(w[2], w[0], w[1])] = s
                     cnt[(w[2], w[0], w[1])] = len(e)
+                    iv[(r,) + tuple(w)] = (b0, s, k)
                 ptr[r] += 1
                 go = True
             for (out, terms, add) in groups[r]:
@@ -147,7 +173,7 @@ def _schedule(calls, groups, cores, topo):
                     go = True
     assert all(ptr[r] == len(calls[r]) for r in R)
     assert all((r,) + gr[0] in eta for r in R for gr in groups[r])
-    return eta, cnt
+    return eta, cnt, iv
 
 
 def rank_program(g, core, T, topo):
@@ -156,10 +182,15 @@ def rank_program(g, core, T, topo):
         return
     MASK, cores, sem = T.tables["MASK"], T.cores, T.sem
     calls, groups = _plan(MASK, cores, topo)
-    eta, cnt = _schedule(calls, groups, cores, topo)
+    eta, cnt, iv = _schedule(calls, groups, cores, topo, set())
     for q in calls:
         calls[q].sort(key=lambda c: max(eta[(q, w[0], w[1])] for w in c))
-    eta, cnt = _schedule(calls, groups, cores, topo)
+    eta, cnt, iv = _schedule(calls, groups, cores, topo, set())
+    wide = set()
+    for key, (a, s, k) in iv.items():
+        if k and not any(o[0] == key[0] and k2 and k2 != k and a2 < s + 0.4 and s2 + 0.4 > a for o, (a2, s2, k2) in iv.items()):
+            wide.add(key[:3])
+    eta, cnt, iv = _schedule(calls, groups, cores, topo, wide)
     tile = {}
     for q in groups:
         for (out, terms, add) in groups[q]:
@@ -178,10 +209,14 @@ def rank_program(g, core, T, topo):
         base = 0 if q == idx else WW
         if kind == "w":
             return T.ws[:, base:base + WW]
+        if kind == "a":
+            return T.ws[:, base:base + WW - M]
+        if kind == "b":
+            return T.ws[:, base + WW - M:base + WW]
         return T.ws[:, base + tile[idx] * M:base + (tile[idx] + 1) * M]
 
     def have(kind, idx):
-        if kind in ("x", "w", "t") and idx == r:
+        if kind in ("x", "w", "t", "a", "b") and idx == r:
             return (sem.lx if kind == "x" else sem.lw), 16
         if (kind, idx) in made:
             return (sem.rp if kind == "p" else sem["rl%d" % idx]), 1
@@ -196,7 +231,7 @@ def rank_program(g, core, T, topo):
     for call in calls[r]:
         kind, idx = call[0][0], call[0][1]
         g.wait_ge(*have(kind, idx))
-        trs, engs = [], _engines(call, r, cores, topo)
+        trs, engs = [], _engines(call, r, cores, topo, wide)
         for e0 in sorted(set(e[0] for e in engs)):
             ws = [(w, e) for w, e in zip(call, engs) if e[0] == e0]
             to = [topo.addr(cores[w[2]], core) for w, e in ws]

@@ -4,117 +4,31 @@ from concourse.mybir import AluOpType
 N, DEG, TK, M = 8, 3, 256, 128
 WW = DEG * M
 NB = 4
+WORLD = 512
+WK = ("w0", "w1", "w2", "w01", "w012")
+NARROW = 2
+SPLIT = 1
 
 SCRATCH = {
     "xs": ("sbuf", [128, N * TK], "bfloat16"),
     "hs": ("sbuf", [128, N * TK], "bfloat16"),
-    "ws": ("sbuf", [128, 2 * WW], "bfloat16"),
-    "po": ("sbuf", [128, TK], "bfloat16"),
-    "pi": ("sbuf", [128, TK], "bfloat16"),
+    "ws": ("sbuf", [128, N * WW], "bfloat16"),
     "zero": ("sbuf", [128, TK], "float32"),
     "yo": ("sbuf", [128, TK], "bfloat16"),
 }
 for _b in range(NB):
     SCRATCH["ps%d" % _b] = ("psum", [128, 512], "float32")
-SEMAPHORES = ["lx", "lw", "z", "snt", "st", "rf", "rp", "ad"] + ["mm%d" % _b for _b in range(NB)]
+SEMAPHORES = ["lx", "lw", "z", "snt", "st", "rf"] + ["mm%d" % _b for _b in range(NB)]
 for _k in range(N):
-    SEMAPHORES += ["ax%d" % _k, "aw%d" % _k, "at%d" % _k, "ap%d" % _k, "ah%d" % _k, "rl%d" % _k, "aa%d" % _k, "ab%d" % _k]
-SIZE = {"x": 1.0, "h": 1.0, "p": 1.0, "w": 1.5, "t": 0.5, "a": 1.0, "b": 0.5}
+    SEMAPHORES += ["rl%d" % _k] + ["a%s_%d" % (_kd, _k) for _kd in ("x", "h") + WK]
+
+
+def _size(kind):
+    return 1.0 if kind in ("x", "h") else 0.5 * (len(kind) - 1)
 
 
 def _bits(m):
     return [e for e in range(m.bit_length()) if (m >> e) & 1]
-
-
-def _plan(MASK, cores, topo):
-    R = range(len(cores))
-
-    def ok(a, b):
-        return a == b or topo.may_write(cores[a], cores[b])
-
-    def near(a, b):
-        return a != b and topo.host(cores[a]) == topo.host(cores[b]) and topo.chip(cores[a]) == topo.chip(cores[b])
-
-    users = {j: [u for u in R if j in MASK[u]] for j in R}
-    hubs = [j for j in R if not all(ok(k, j) for k in MASK[j])]
-    far_tile = {j: [i for i, k in enumerate(MASK[j]) if not ok(k, j)] for j in hubs}
-    assert all(len(far_tile[j]) == 1 for j in hubs)
-    groups = {r: [] for r in R}
-    first, second, third = {r: [] for r in R}, {r: [] for r in R}, {r: [] for r in R}
-
-    def full(j, r, two=False):
-        groups[r].append((("h", j), [((("a" if i < DEG - 1 else "b") if two else "w", j), i, ("x", k)) for i, k in enumerate(MASK[j])], None))
-
-    maker, split = {}, {}
-    for j in R:
-        if j not in hubs:
-            maker[j] = j
-            continue
-        c = [p for p in R if ok(j, p) and all(ok(k, p) for k in MASK[j])]
-        maker[j] = min(c, key=lambda p: (len([u for u in users[p] if u != p and not near(p, u)]), p))
-        split[j] = [u for u in users[j] if u != j and not ok(maker[j], u)]
-    for r in R:
-        full(r, r)
-    again = [(j, k) for k in hubs for j in MASK[k] if j not in hubs and set(MASK[j]) <= set(MASK[k]) and ok(j, k)]
-    for (j, k) in again:
-        full(j, k)
-    for j in hubs:
-        full(j, maker[j], True)
-        i = far_tile[j][0]
-        for u in split[j]:
-            groups[u].append((("h", j), [(("t", j), i, ("x", MASK[j][i]))], ("p", j)))
-        if split[j]:
-            groups[j].insert(0, (("p", j), [(("w", j), a, ("x", k)) for a, k in enumerate(MASK[j]) if a != i], None))
-    want = {k: set() for k in R}
-    for r in R:
-        for (out, terms, add) in groups[r]:
-            for (wk, i, rhs) in terms:
-                if rhs[1] != r:
-                    want[rhs[1]].add(r)
-    for k in R:
-        direct = sorted(u for u in want[k] if ok(k, u))
-        if k in hubs:
-            heads = []
-            for u in direct:
-                mate = [v for v in direct if near(u, v)]
-                if not mate or u == maker[k] or (mate[0] != maker[k] and maker.get(MASK[k][far_tile[k][0]]) != u and
-                                                 (maker.get(MASK[k][far_tile[k][0]]) == mate[0] or u < mate[0])):
-                    heads.append(u)
-            heads.sort(key=lambda u: (u != maker[k], u))
-            first[k].append([("x", k, u) for u in heads])
-            relay_to = [u for u in want[k] if not ok(k, u)]
-            for n, u in enumerate(heads):
-                pas = [("x", k, v) for v in direct if near(u, v) and v not in heads]
-                if n == 0:
-                    assert all(ok(u, v) for v in relay_to)
-                    pas = [("x", k, v) for v in relay_to] + pas
-                if pas:
-                    second[u].append(pas)
-            nb = [v for v in R if near(k, v) and ok(v, maker[k])][0]
-            first[k].append([("b", k, nb)])
-            second[nb].append([("b", k, maker[k])])
-            first[k].append([("a", k, maker[k])])
-            for u in split[k]:
-                first[k].append([("t", k, u)])
-                third[k].append([("p", k, u)])
-        elif direct:
-            assert len(direct) == len(want[k])
-            first[k].append([("x", k, u) for u in sorted(direct, key=lambda u: (u not in hubs, near(k, u), u))])
-            for (j, u) in again:
-                if j == k:
-                    first[k].append([("w", k, u)])
-    for j in R:
-        to = [u for u in users[j] if u != maker[j] and ("h", j) not in [gr[0] for gr in groups[u]]]
-        if to:
-            assert all(ok(maker[j], u) for u in to)
-            third[maker[j]].append([("h", j, u) for u in sorted(to, key=lambda u: (near(maker[j], u), u))])
-    for r in R:
-        groups[r].append((("y", r), [(("w", r), i, ("h", j)) for i, j in enumerate(MASK[r])], None))
-    calls = {r: first[r] + second[r] + third[r] for r in R}
-    for r in R:
-        for c in calls[r]:
-            assert all(ok(r, w[2]) and w[2] != r for w in c)
-    return calls, groups
 
 
 def _link(a, b, topo):
@@ -123,29 +37,120 @@ def _link(a, b, topo):
     return 1 if topo.rack(topo.host(a)) != topo.rack(topo.host(b)) else 2
 
 
-def _engines(call, r, cores, topo, wide):
-    me = cores[r]
-    leave = min([_bits(topo.mask(me, c)) for c in cores if c != me and topo.mask(me, c)], key=len)
+def _plan(MASK, cores, topo):
+    allc = list(cores)
+    car = {}
+    for r, c in enumerate(cores):
+        key = (topo.host(c), topo.chip(c))
+        if key not in car:
+            oth = [d for d in range(WORLD) if (topo.host(d), topo.chip(d)) == key and topo.die(d) != topo.die(c)]
+            car[key] = (len(allc), len(allc) + 1)
+            allc += [oth[0], oth[-1]]
+    A = lambda r: car[(topo.host(cores[r]), topo.chip(cores[r]))][0]
+    B = lambda r: car[(topo.host(cores[r]), topo.chip(cores[r]))][1]
+    makes = {0: [0, 6], 1: [1, 2], 2: [2, 5], 3: [3, 4], 4: [4], 5: [5, 2, 6], 6: [6, 0], 7: [7]}
+    calls = {a: [] for a in range(len(allc))}
+    lag = {}
+
+    def send(a, *ws):
+        calls[a].append([tuple(w) for w in ws])
+
+    def xsend(k, *to):
+        ws = [("x", k, u) for u in to]
+        far = [w for w in ws if _link(allc[k], allc[w[2]], topo) == 1]
+        if SPLIT and far and len(far) < len(ws):
+            send(k, *far)
+            send(k, *[w for w in ws if w not in far])
+            lag[(k,) + calls[k][-1][0]] = 0.35
+        else:
+            send(k, *ws)
+
+    def carried(j, to, p1, c1, p2, c2, direct):
+        if p2:
+            send(j, (p1, j, c1), (p2, j, c2))
+            send(c2, (p2, j, to))
+        else:
+            send(j, (p1, j, c1))
+        send(c1, (p1, j, to))
+        send(j, (direct, j, to))
+        lag[(j,) + calls[j][-1][0]] = 0.4
+
+    xsend(0, 6, 1)
+    xsend(1, 3, 7, 0)
+    xsend(2, 5, 1, 3)
+    xsend(4, 3)
+    xsend(5, 2, 7, 4)
+    xsend(6, 0, 5)
+    carried(0, 6, "w0", A(0), "w1", B(0), "w2")
+    carried(2, 5, "w0", 3, "w1", A(2), "w2")
+    carried(6, 0, "w0", 7, "w1", A(6), "w2")
+    carried(4, 3, "w01", A(4), None, None, "w2")
+    carried(5, 2, "w01", B(5), None, None, "w2")
+    send(2, ("w012", 2, 1))
+    lag[(2, "w012", 2, 1)] = 0.45
+    send(6, ("w012", 6, 5))
+    lag[(6, "w012", 6, 5)] = 0.45
+    send(0, ("x", 6, 2), ("x", 6, 1))
+    send(1, ("x", 2, 0))
+    send(2, ("x", 5, 1), ("x", 5, 3))
+    send(5, ("x", 2, 6), ("x", 2, 4))
+    send(6, ("x", 0, 5))
+    send(7, ("x", 1, 6))
+    send(0, ("h", 0, 1))
+    send(0, ("h", 6, 2))
+    send(1, ("h", 1, 7), ("h", 1, 3), ("h", 1, 0))
+    send(5, ("h", 2, 6), ("h", 2, 4))
+    send(5, ("h", 5, 7), ("h", 5, 4))
+    got = {a: set() for a in calls}
+    for a in calls:
+        for c in calls[a]:
+            for (kd, i, to) in c:
+                assert to != a and topo.may_write(allc[a], allc[to]) and (kd, i) not in got[to], (a, kd, i, to)
+                got[to].add((kd, i))
+    groups = {r: [] for r in range(len(cores))}
+    for r in groups:
+        for j in makes[r]:
+            terms = []
+            for i, k in enumerate(MASK[j]):
+                wk = [("w012", r)] if j == r else [(kd, q) for (kd, q) in got[r] if q == j and kd[0] == "w" and str(i) in kd]
+                assert len(wk) == 1 and (k == r or ("x", k) in got[r]), (r, j, i)
+                terms.append((wk[0], i, ("x", k)))
+            groups[r].append((("h", j), terms))
+        assert all(j in makes[r] or ("h", j) in got[r] for j in MASK[r]), r
+        groups[r].append((("y", r), [(("w012", r), i, ("h", j)) for i, j in enumerate(MASK[r])]))
+    return allc, calls, groups, lag
+
+
+def _engines(call, a, allc, topo, wide):
+    me = allc[a]
+    leave = min([_bits(topo.mask(me, c)) for c in allc if c != me and topo.mask(me, c)], key=len)
+    here = []
+    for w in call:
+        if _link(me, allc[w[2]], topo) == 0 and w[:2] not in here:
+            here.append(w[:2])
     out = []
     for w in call:
-        k, m = _link(me, cores[w[2]], topo), _bits(topo.mask(me, cores[w[2]]))
+        k, m = _link(me, allc[w[2]], topo), _bits(topo.mask(me, allc[w[2]]))
         if k == 0:
-            out.append([e for e in m if e not in leave])
-        elif (r, w[0], w[1]) in wide:
+            stay = [e for e in m if e not in leave]
+            n = len(stay) // (1 if len(here) == 1 else 2 if len(here) == 2 else 4)
+            i = here.index(w[:2])
+            out.append(stay[i * n:(i + 1) * n])
+        elif (a, w[0], w[1]) in wide:
             out.append(m)
         else:
             out.append(m[k % 2::2])
     return out
 
 
-def _schedule(calls, groups, cores, topo, wide):
-    R = range(len(cores))
+def _schedule(calls, groups, allc, topo, wide):
+    R = range(len(allc))
     eta, cnt, iv = {}, {}, {}
-    for r in R:
+    for r in groups:
         eta[(r, "x", r)] = 0.0
-        for kd in "wtab":
+        for kd in WK:
             eta[(r, kd, r)] = 0.3
-    ptr, tq, busy = [0] * len(cores), [0.0] * len(cores), [{} for r in R]
+    ptr, tq, busy = [0] * len(allc), [0.0] * len(allc), [{} for r in R]
     go = True
     while go:
         go = False
@@ -154,11 +159,11 @@ def _schedule(calls, groups, cores, topo, wide):
                 call = calls[r][ptr[r]]
                 t = max([tq[r]] + [eta[(r, w[0], w[1])] for w in call])
                 tq[r] = t + 0.3
-                for w, e in zip(call, _engines(call, r, cores, topo, wide)):
+                for w, e in zip(call, _engines(call, r, allc, topo, wide)):
                     assert (w[2], w[0], w[1]) not in eta, w
-                    k = _link(cores[r], cores[w[2]], topo)
+                    k = _link(allc[r], allc[w[2]], topo)
                     b0 = max([t + 1.0] + [busy[r].get(b, 0.0) for b in e])
-                    s = b0 + SIZE[w[0]] * (0.3, 2.0, 0.5)[k]
+                    s = b0 + _size(w[0]) * (0.3, 2.0, 0.5)[k]
                     for b in e:
                         busy[r][b] = s
                     eta[(w[2], w[0], w[1])] = s
@@ -166,86 +171,85 @@ def _schedule(calls, groups, cores, topo, wide):
                     iv[(r,) + tuple(w)] = (b0, s, k)
                 ptr[r] += 1
                 go = True
-            for (out, terms, add) in groups[r]:
-                ins = [(r,) + t[0] for t in terms] + [(r,) + t[2] for t in terms] + ([(r,) + add] if add else [])
+            for (out, terms) in groups.get(r, []):
+                ins = [(r,) + t[0] for t in terms] + [(r,) + t[2] for t in terms]
                 if (r,) + out not in eta and all(i in eta for i in ins):
                     eta[(r,) + out] = max(eta[i] for i in ins) + 0.5
                     go = True
     assert all(ptr[r] == len(calls[r]) for r in R)
-    assert all((r,) + gr[0] in eta for r in R for gr in groups[r])
+    assert all((r,) + gr[0] in eta for r in groups for gr in groups[r])
     return eta, cnt, iv
 
 
-def rank_program(g, core, T, topo):
-    r = T.rank_of(core)
-    if r is None:
-        return
-    MASK, cores, sem = T.tables["MASK"], T.cores, T.sem
-    calls, groups = _plan(MASK, cores, topo)
-    eta, cnt, iv = _schedule(calls, groups, cores, topo, set())
+def _build(MASK, cores, topo):
+    allc, calls, groups, lag = _plan(MASK, cores, topo)
+    eta, cnt, iv = _schedule(calls, groups, allc, topo, set())
     for q in calls:
-        calls[q].sort(key=lambda c: max(eta[(q, w[0], w[1])] for w in c))
-    eta, cnt, iv = _schedule(calls, groups, cores, topo, set())
+        calls[q].sort(key=lambda c: max(eta[(q, w[0], w[1])] for w in c) + lag.get((q,) + c[0], 0.0))
+    eta, cnt, iv = _schedule(calls, groups, allc, topo, set())
     wide = set()
     for key, (a, s, k) in iv.items():
         if k and not any(o[0] == key[0] and k2 and k2 != k and a2 < s + 0.4 and s2 + 0.4 > a for o, (a2, s2, k2) in iv.items()):
-            wide.add(key[:3])
-    eta, cnt, iv = _schedule(calls, groups, cores, topo, wide)
-    tile = {}
-    for q in groups:
-        for (out, terms, add) in groups[q]:
-            for (wk, i, rhs) in terms:
-                if wk[0] == "t":
-                    tile[wk[1]] = i
-    made = [gr[0] for gr in groups[r]]
+            if not (NARROW >= 1 and key[1][0] == "w") and not (NARROW >= 2 and k == 1):
+                wide.add(key[:3])
+    eta, cnt, iv = _schedule(calls, groups, allc, topo, wide)
+    return allc, calls, groups, eta, cnt, iv, wide
 
-    def buf(q, kind, idx):
+
+def rank_program(g, core, T, topo):
+    MASK, cores, sem = T.tables["MASK"], T.cores, T.sem
+    allc, calls, groups, eta, cnt, iv, wide = _build(MASK, cores, topo)
+    if core not in allc:
+        return
+    r = allc.index(core)
+    made = [gr[0] for gr in groups.get(r, [])]
+
+    def buf(kind, idx):
         if kind == "x":
             return T.xs[:, idx * TK:(idx + 1) * TK]
         if kind == "h":
             return T.hs[:, idx * TK:(idx + 1) * TK]
-        if kind == "p":
-            return T.po[:] if q == idx else T.pi[:]
-        base = 0 if q == idx else WW
-        if kind == "w":
-            return T.ws[:, base:base + WW]
-        if kind == "a":
-            return T.ws[:, base:base + WW - M]
-        if kind == "b":
-            return T.ws[:, base + WW - M:base + WW]
-        return T.ws[:, base + tile[idx] * M:base + (tile[idx] + 1) * M]
+        return T.ws[:, idx * WW + int(kind[1]) * M:idx * WW + (int(kind[-1]) + 1) * M]
 
     def have(kind, idx):
-        if kind in ("x", "w", "t", "a", "b") and idx == r:
+        if kind != "h" and idx == r:
             return (sem.lx if kind == "x" else sem.lw), 16
         if (kind, idx) in made:
-            return (sem.rp if kind == "p" else sem["rl%d" % idx]), 1
-        return sem["a%s%d" % (kind, idx)], cnt[(r, kind, idx)]
+            return sem["rl%d" % idx], 1
+        return sem["a%s_%d" % (kind, idx)], cnt[(r, kind, idx)]
 
-    g.sync.dma_start(buf(r, "x", r), T.x[:]).then_inc(sem.lx, 16)
-    g.scalar.dma_start(buf(r, "w", r), T.w[:]).then_inc(sem.lw, 16)
-    g.vector.memset(T.zero[:], 0.0).then_inc(sem.z, 1)
-    g.vector.wait_ge(sem.z, 1)
+    if r in groups:
+        g.sync.dma_start(buf("x", r), T.x[:]).then_inc(sem.lx, 16)
+        g.scalar.dma_start(buf("w012", r), T.w[:]).then_inc(sem.lw, 16)
+        g.vector.memset(T.zero[:], 0.0).then_inc(sem.z, 1)
+        g.vector.wait_ge(sem.z, 1)
 
     total = 0
     for call in calls[r]:
-        kind, idx = call[0][0], call[0][1]
-        g.wait_ge(*have(kind, idx))
-        trs, engs = [], _engines(call, r, cores, topo, wide)
-        for e0 in sorted(set(e[0] for e in engs)):
-            ws = [(w, e) for w, e in zip(call, engs) if e[0] == e0]
-            to = [topo.addr(cores[w[2]], core) for w, e in ws]
+        engs = _engines(call, r, allc, topo, wide)
+        keys = []
+        for w, e in zip(call, engs):
+            if (w[0], w[1], e[0]) not in keys:
+                keys.append((w[0], w[1], e[0]))
+        for it in sorted(set(k[:2] for k in keys)):
+            g.wait_ge(*have(*it))
+        trs = []
+        for (kind, idx, e0) in keys:
+            ws = [(w, e) for w, e in zip(call, engs) if (w[0], w[1], e[0]) == (kind, idx, e0)]
+            to = [topo.addr(allc[w[2]], core) for w, e in ws]
             trs.append(RemoteDMATransfer(dst_ids=[DstId(rid=a, pnc=b) for a, b in to],
                                          dma_engine_mask=sum(1 << b for b in ws[0][1]),
-                                         remote_sem=sem["a%s%d" % (kind, idx)], srcs=[buf(r, kind, idx)],
-                                         dsts=[buf(w[2], kind, idx) for w, e in ws]))
+                                         remote_sem=sem["a%s_%d" % (kind, idx)], srcs=[buf(kind, idx)],
+                                         dsts=[buf(kind, idx) for w, e in ws]))
             total += len(ws[0][1])
         g.remote_dma_fused(trs, local_sem=sem.snt)
     if total:
         g.wait_ge(sem.snt, total)
+    if r not in groups:
+        return
 
     mms = []
-    for b, (out, terms, add) in enumerate(groups[r]):
+    for b, (out, terms) in enumerate(groups[r]):
         for (wk, i, rhs) in terms:
             mms.append((max(eta[(r,) + wk], eta[(r,) + rhs]), b, i, wk, rhs))
     mms.sort()
@@ -256,25 +260,19 @@ def rank_program(g, core, T, topo):
             if it not in seen:
                 g.tensor.wait_ge(*have(*it))
                 seen.add(it)
-        s = (0 if wk[1] == r else WW) + i * M
+        s = wk[1] * WW + i * M
         left[b] -= 1
-        ins = g.tensor.matmul(T["ps%d" % b][:, 0:TK], T.ws[:, s:s + M], buf(r, *rhs), left[b] == size[b] - 1, left[b] == 0)
+        ins = g.tensor.matmul(T["ps%d" % b][:, 0:TK], T.ws[:, s:s + M], buf(*rhs), left[b] == size[b] - 1, left[b] == 0)
         if left[b] == 0:
             ins.then_inc(sem["mm%d" % b], 1)
     for b in sorted(range(len(groups[r])), key=lambda b: eta[(r,) + groups[r][b][0]]):
-        out, terms, add = groups[r][b]
+        out, terms = groups[r][b]
         ps = T["ps%d" % b][:, 0:TK]
         g.vector.wait_ge(sem["mm%d" % b], 1)
-        if add:
-            g.vector.wait_ge(*have(*add))
-            g.vector.tensor_tensor(ps, ps, buf(r, *add), AluOpType.add).then_inc(sem.ad, 1)
-            g.vector.wait_ge(sem.ad, 1)
-        if out[0] == "p":
-            g.vector.tensor_copy(buf(r, *out), ps).then_inc(sem.rp, 1)
-        elif out[0] == "y":
+        if out[0] == "y":
             g.vector.tensor_tensor(T.yo[:], ps, T.zero[:], AluOpType.max).then_inc(sem.rf, 1)
         else:
-            g.vector.tensor_tensor(buf(r, *out), ps, T.zero[:], AluOpType.max).then_inc(sem["rl%d" % out[1]], 1)
+            g.vector.tensor_tensor(buf(*out), ps, T.zero[:], AluOpType.max).then_inc(sem["rl%d" % out[1]], 1)
     g.sync.wait_ge(sem.rf, 1)
     g.sync.dma_start(T.y[:], T.yo[:]).then_inc(sem.st, 16)
     g.sync.wait_ge(sem.st, 16)

from concourse.bass import DstId, RemoteDMATransfer
from concourse.mybir import AluOpType

N, DEG, TK, M = 8, 3, 256, 128
WW = DEG * M
NB = 4
WORLD = 512
WK = ("w0", "w1", "w2", "w01", "w012")
NARROW = 2
SPLIT = 1

SCRATCH = {
    "xs": ("sbuf", [128, N * TK], "bfloat16"),
    "hs": ("sbuf", [128, N * TK], "bfloat16"),
    "ws": ("sbuf", [128, N * WW], "bfloat16"),
    "zero": ("sbuf", [128, TK], "float32"),
    "yo": ("sbuf", [128, TK], "bfloat16"),
}
for _b in range(NB):
    SCRATCH["ps%d" % _b] = ("psum", [128, 512], "float32")
SEMAPHORES = ["lx", "lw", "z", "snt", "st", "rf"] + ["mm%d" % _b for _b in range(NB)]
for _k in range(N):
    SEMAPHORES += ["rl%d" % _k] + ["a%s_%d" % (_kd, _k) for _kd in ("x", "h") + WK]


def _size(kind):
    return 1.0 if kind in ("x", "h") else 0.5 * (len(kind) - 1)


def _bits(m):
    return [e for e in range(m.bit_length()) if (m >> e) & 1]


def _link(a, b, topo):
    if topo.host(a) == topo.host(b) and topo.chip(a) == topo.chip(b):
        return 0
    return 1 if topo.rack(topo.host(a)) != topo.rack(topo.host(b)) else 2


def _plan(MASK, cores, topo):
    allc = list(cores)
    car = {}
    for r, c in enumerate(cores):
        key = (topo.host(c), topo.chip(c))
        if key not in car:
            oth = [d for d in range(WORLD) if (topo.host(d), topo.chip(d)) == key and topo.die(d) != topo.die(c)]
            car[key] = (len(allc), len(allc) + 1)
            allc += [oth[0], oth[-1]]
    A = lambda r: car[(topo.host(cores[r]), topo.chip(cores[r]))][0]
    B = lambda r: car[(topo.host(cores[r]), topo.chip(cores[r]))][1]
    makes = {0: [0, 6], 1: [1, 2], 2: [2, 5], 3: [3, 4], 4: [4], 5: [5, 2, 6], 6: [6, 0], 7: [7]}
    calls = {a: [] for a in range(len(allc))}
    lag = {}

    def send(a, *ws):
        calls[a].append([tuple(w) for w in ws])

    def xsend(k, *to):
        ws = [("x", k, u) for u in to]
        far = [w for w in ws if _link(allc[k], allc[w[2]], topo) == 1]
        if SPLIT and far and len(far) < len(ws):
            send(k, *far)
            send(k, *[w for w in ws if w not in far])
            lag[(k,) + calls[k][-1][0]] = 0.35
        else:
            send(k, *ws)

    def carried(j, to, p1, c1, p2, c2, direct):
        if p2:
            send(j, (p1, j, c1), (p2, j, c2))
            send(c2, (p2, j, to))
        else:
            send(j, (p1, j, c1))
        send(c1, (p1, j, to))
        send(j, (direct, j, to))
        lag[(j,) + calls[j][-1][0]] = 0.4

    xsend(0, 6, 1)
    xsend(1, 3, 7, 0)
    xsend(2, 5, 1, 3)
    xsend(4, 3)
    xsend(5, 2, 7, 4)
    xsend(6, 0, 5)
    carried(0, 6, "w0", A(0), "w1", B(0), "w2")
    carried(2, 5, "w0", 3, "w1", A(2), "w2")
    carried(6, 0, "w0", 7, "w1", A(6), "w2")
    carried(4, 3, "w01", A(4), None, None, "w2")
    carried(5, 2, "w01", B(5), None, None, "w2")
    send(2, ("w012", 2, 1))
    lag[(2, "w012", 2, 1)] = 0.45
    send(6, ("w012", 6, 5))
    lag[(6, "w012", 6, 5)] = 0.45
    send(0, ("x", 6, 2), ("x", 6, 1))
    send(1, ("x", 2, 0))
    send(2, ("x", 5, 1), ("x", 5, 3))
    send(5, ("x", 2, 6), ("x", 2, 4))
    send(6, ("x", 0, 5))
    send(7, ("x", 1, 6))
    send(0, ("h", 0, 1))
    send(0, ("h", 6, 2))
    send(1, ("h", 1, 7), ("h", 1, 3), ("h", 1, 0))
    send(5, ("h", 2, 6), ("h", 2, 4))
    send(5, ("h", 5, 7), ("h", 5, 4))
    got = {a: set() for a in calls}
    for a in calls:
        for c in calls[a]:
            for (kd, i, to) in c:
                assert to != a and topo.may_write(allc[a], allc[to]) and (kd, i) not in got[to], (a, kd, i, to)
                got[to].add((kd, i))
    groups = {r: [] for r in range(len(cores))}
    for r in groups:
        for j in makes[r]:
            terms = []
            for i, k in enumerate(MASK[j]):
                wk = [("w012", r)] if j == r else [(kd, q) for (kd, q) in got[r] if q == j and kd[0] == "w" and str(i) in kd]
                assert len(wk) == 1 and (k == r or ("x", k) in got[r]), (r, j, i)
                terms.append((wk[0], i, ("x", k)))
            groups[r].append((("h", j), terms))
        assert all(j in makes[r] or ("h", j) in got[r] for j in MASK[r]), r
        groups[r].append((("y", r), [(("w012", r), i, ("h", j)) for i, j in enumerate(MASK[r])]))
    return allc, calls, groups, lag


def _engines(call, a, allc, topo, wide):
    me = allc[a]
    leave = min([_bits(topo.mask(me, c)) for c in allc if c != me and topo.mask(me, c)], key=len)
    here = []
    for w in call:
        if _link(me, allc[w[2]], topo) == 0 and w[:2] not in here:
            here.append(w[:2])
    out = []
    for w in call:
        k, m = _link(me, allc[w[2]], topo), _bits(topo.mask(me, allc[w[2]]))
        if k == 0:
            stay = [e for e in m if e not in leave]
            n = len(stay) // (1 if len(here) == 1 else 2 if len(here) == 2 else 4)
            i = here.index(w[:2])
            out.append(stay[i * n:(i + 1) * n])
        elif (a, w[0], w[1]) in wide:
            out.append(m)
        else:
            out.append(m[k % 2::2])
    return out


def _schedule(calls, groups, allc, topo, wide):
    R = range(len(allc))
    eta, cnt, iv = {}, {}, {}
    for r in groups:
        eta[(r, "x", r)] = 0.0
        for kd in WK:
            eta[(r, kd, r)] = 0.3
    ptr, tq, busy = [0] * len(allc), [0.0] * len(allc), [{} for r in R]
    go = True
    while go:
        go = False
        for r in R:
            while ptr[r] < len(calls[r]) and all((r, w[0], w[1]) in eta for w in calls[r][ptr[r]]):
                call = calls[r][ptr[r]]
                t = max([tq[r]] + [eta[(r, w[0], w[1])] for w in call])
                tq[r] = t + 0.3
                for w, e in zip(call, _engines(call, r, allc, topo, wide)):
                    assert (w[2], w[0], w[1]) not in eta, w
                    k = _link(allc[r], allc[w[2]], topo)
                    b0 = max([t + 1.0] + [busy[r].get(b, 0.0) for b in e])
                    s = b0 + _size(w[0]) * (0.3, 2.0, 0.5)[k]
                    for b in e:
                        busy[r][b] = s
                    eta[(w[2], w[0], w[1])] = s
                    cnt[(w[2], w[0], w[1])] = len(e)
                    iv[(r,) + tuple(w)] = (b0, s, k)
                ptr[r] += 1
                go = True
            for (out, terms) in groups.get(r, []):
                ins = [(r,) + t[0] for t in terms] + [(r,) + t[2] for t in terms]
                if (r,) + out not in eta and all(i in eta for i in ins):
                    eta[(r,) + out] = max(eta[i] for i in ins) + 0.5
                    go = True
    assert all(ptr[r] == len(calls[r]) for r in R)
    assert all((r,) + gr[0] in eta for r in groups for gr in groups[r])
    return eta, cnt, iv


def _build(MASK, cores, topo):
    allc, calls, groups, lag = _plan(MASK, cores, topo)
    eta, cnt, iv = _schedule(calls, groups, allc, topo, set())
    for q in calls:
        calls[q].sort(key=lambda c: max(eta[(q, w[0], w[1])] for w in c) + lag.get((q,) + c[0], 0.0))
    eta, cnt, iv = _schedule(calls, groups, allc, topo, set())
    wide = set()
    for key, (a, s, k) in iv.items():
        if k and not any(o[0] == key[0] and k2 and k2 != k and a2 < s + 0.4 and s2 + 0.4 > a for o, (a2, s2, k2) in iv.items()):
            if not (NARROW >= 1 and key[1][0] == "w") and not (NARROW >= 2 and k == 1):
                wide.add(key[:3])
    eta, cnt, iv = _schedule(calls, groups, allc, topo, wide)
    return allc, calls, groups, eta, cnt, iv, wide


def rank_program(g, core, T, topo):
    MASK, cores, sem = T.tables["MASK"], T.cores, T.sem
    allc, calls, groups, eta, cnt, iv, wide = _build(MASK, cores, topo)
    if core not in allc:
        return
    r = allc.index(core)
    made = [gr[0] for gr in groups.get(r, [])]

    def buf(kind, idx):
        if kind == "x":
            return T.xs[:, idx * TK:(idx + 1) * TK]
        if kind == "h":
            return T.hs[:, idx * TK:(idx + 1) * TK]
        return T.ws[:, idx * WW + int(kind[1]) * M:idx * WW + (int(kind[-1]) + 1) * M]

    def have(kind, idx):
        if kind != "h" and idx == r:
            return (sem.lx if kind == "x" else sem.lw), 16
        if (kind, idx) in made:
            return sem["rl%d" % idx], 1
        return sem["a%s_%d" % (kind, idx)], cnt[(r, kind, idx)]

    if r in groups:
        g.sync.dma_start(buf("x", r), T.x[:]).then_inc(sem.lx, 16)
        g.scalar.dma_start(buf("w012", r), T.w[:]).then_inc(sem.lw, 16)
        g.vector.memset(T.zero[:], 0.0).then_inc(sem.z, 1)
        g.vector.wait_ge(sem.z, 1)

    total = 0
    for call in calls[r]:
        engs = _engines(call, r, allc, topo, wide)
        keys = []
        for w, e in zip(call, engs):
            if (w[0], w[1], e[0]) not in keys:
                keys.append((w[0], w[1], e[0]))
        for it in sorted(set(k[:2] for k in keys)):
            g.wait_ge(*have(*it))
        trs = []
        for (kind, idx, e0) in keys:
            ws = [(w, e) for w, e in zip(call, engs) if (w[0], w[1], e[0]) == (kind, idx, e0)]
            to = [topo.addr(allc[w[2]], core) for w, e in ws]
            trs.append(RemoteDMATransfer(dst_ids=[DstId(rid=a, pnc=b) for a, b in to],
                                         dma_engine_mask=sum(1 << b for b in ws[0][1]),
                                         remote_sem=sem["a%s_%d" % (kind, idx)], srcs=[buf(kind, idx)],
                                         dsts=[buf(kind, idx) for w, e in ws]))
            total += len(ws[0][1])
        g.remote_dma_fused(trs, local_sem=sem.snt)
    if total:
        g.wait_ge(sem.snt, total)
    if r not in groups:
        return

    mms = []
    for b, (out, terms) in enumerate(groups[r]):
        for (wk, i, rhs) in terms:
            mms.append((max(eta[(r,) + wk], eta[(r,) + rhs]), b, i, wk, rhs))
    mms.sort()
    size = [len(gr[1]) for gr in groups[r]]
    left, seen = list(size), set()
    for (t, b, i, wk, rhs) in mms:
        for it in (wk, rhs):
            if it not in seen:
                g.tensor.wait_ge(*have(*it))
                seen.add(it)
        s = wk[1] * WW + i * M
        left[b] -= 1
        ins = g.tensor.matmul(T["ps%d" % b][:, 0:TK], T.ws[:, s:s + M], buf(*rhs), left[b] == size[b] - 1, left[b] == 0)
        if left[b] == 0:
            ins.then_inc(sem["mm%d" % b], 1)
    for b in sorted(range(len(groups[r])), key=lambda b: eta[(r,) + groups[r][b][0]]):
        out, terms = groups[r][b]
        ps = T["ps%d" % b][:, 0:TK]
        g.vector.wait_ge(sem["mm%d" % b], 1)
        if out[0] == "y":
            g.vector.tensor_tensor(T.yo[:], ps, T.zero[:], AluOpType.max).then_inc(sem.rf, 1)
        else:
            g.vector.tensor_tensor(buf(*out), ps, T.zero[:], AluOpType.max).then_inc(sem["rl%d" % out[1]], 1)
    g.sync.wait_ge(sem.rf, 1)
    g.sync.dma_start(T.y[:], T.yo[:]).then_inc(sem.st, 16)
    g.sync.wait_ge(sem.st, 16)
